import numpy as np, ml_dtypes
CORES = [6,15,38,47]
N = 4
import mx_ref
BF = ml_dtypes.bfloat16
def gentries(a):
    return np.ascontiguousarray(a.reshape(8, 16, -1).transpose(0, 2, 1)).reshape(8, -1)
def gtable(e):
    e = np.asarray(e); return np.ascontiguousarray(e.reshape(8, -1, 16).transpose(0, 2, 1)).reshape(128, -1).astype(np.int32)
def gcols(t, e):
    v = np.concatenate([t.reshape(8, 16, -1, 4), np.zeros((8, 16, 1, 4), BF)], axis=2)
    return np.ascontiguousarray(np.stack([v[g][:, e[g]] for g in range(8)])).reshape(128, -1)
def f(rng, *shape):
    return mx_ref.flush((rng.standard_normal(shape, dtype=np.float32) * np.exp2(rng.integers(-2, 3, shape[:-1] + (1,)))).astype(BF))
def wide(rng, *shape, cols=0):
    v = rng.standard_normal(shape, dtype=np.float32) * np.exp2(rng.integers(-12, 13, shape)).astype(np.float32)
    if cols: v *= np.repeat(np.exp2(rng.integers(-cols, cols + 1, shape[:-2] + (1, shape[-1] // 4))) * (rng.random(shape[:-2] + (1, shape[-1] // 4)) > 0.0625), 4, axis=-1).astype(np.float32)
    return mx_ref.flush(v.astype(BF))
T, O, K = 256, 4, 256
def lists(rng, alike=False, groups=False, ends=False, few=False):
    c = []
    for r in range(N):
        e = rng.integers(0, K, (8, O, 2, 128))
        if groups: e = np.stack([e[0]] * 8)
        if ends: e = rng.permuted(np.resize([0, K - 1], (8, O, 2, 128)), axis=3)
        if few:
            for m in range(2): e[:, :, m] = rng.permutation(np.resize(rng.permutation(K)[:8], 8 * O * 128)).reshape(8, O, 128)
        c.append(gtable(e.reshape(8, -1)))
    if alike: c = [c[0]] * N
    return np.stack(c)
def setup_inputs(rng):
    return {"x": f(rng, N, 128, 4 * T), "book": np.stack([f(rng, 128, 8 * K)] * N), "cw": lists(rng)}
def setup_inputs_alike(rng):
    d = setup_inputs(rng); d["cw"] = lists(rng, alike=True); return d
def setup_inputs_groups(rng):
    d = setup_inputs(rng); d["cw"] = lists(rng, groups=True); return d
def setup_inputs_ends(rng):
    d = setup_inputs(rng); d["cw"] = lists(rng, ends=True); return d
def setup_inputs_few(rng):
    d = setup_inputs(rng); d["cw"] = lists(rng, few=True); return d
def setup_inputs_spread(rng):
    d = setup_inputs(rng); d["x"] = wide(rng, N, 128, 4 * T, cols=8); d["book"] = np.stack([wide(rng, 128, 8 * K, cols=4)] * N); return d
def check_inputs(d):
    b = []
    for r in range(N):
        if d["cw"][r].min() < 0 or d["cw"][r].max() >= K: b.append("cw")
        if d["book"][r].tobytes() != d["book"][0].tobytes(): b.append("book")
    return b
def reference(x, book, cw):
    W = []
    for s in range(N):
        e = gentries(cw[s])
        for o in range(O):
            a, b = [gcols(np.ascontiguousarray(book[s][:, 4 * K * m:4 * K * m + 4 * K]), e[:, (2 * o + m) * 128:(2 * o + m) * 128 + 128]).astype(np.float32) for m in range(2)]
            W.append(mx_ref.quantize((a + b).astype(BF)))
    y = np.zeros((N, 128, N * O * T), np.float32)
    for r in range(N):
        X = mx_ref.quantize(np.ascontiguousarray(x[r]))
        for i in range(N * O): y[r][:, T * i:T * i + T] = mx_ref.matmul(W[i], X)
    return {"y": y}

@@ -1,0 +1,207 @@
+from concourse.bass import DstId, RemoteDMATransfer
+from concourse.mybir import dt, AluOpType, ActivationFunctionType
+
+N, TC, O, K = 4, 256, 4, 256
+CW = 128
+C = 2
+UC = 2 * CW
+NT = 4
+CFG = {
+    "codes": {0: [(None, ("mate", "plane"))], 1: [(None, ("mate",))]},
+    "lists": {0: [(None, ("diag",))], 1: [(None, ("plane", "diag"))]},
+    "gotpos": {0: 14, 1: 15, 2: 20},
+    "lag": 1, "sl": 2,
+    "evS": (1, 0, 1, 1, 1, 0, 1, 1, 1, 0, 1, 1, 1, 0, 0, 1),
+    "so": [("l", 0), ("l", 1), ("r", 0), ("r", 1)],
+    "half": 0,
+}
+
+SCRATCH = {
+    "cwb": ("sbuf", [128, O, 2, 8], "int32"),
+    "bk0": ("sbuf", [128, NT * K], "bfloat16"),
+    "bk1": ("sbuf", [128, NT * K], "bfloat16"),
+    "xb": ("sbuf", [128, NT * TC], "bfloat16"),
+    "xq": ("sbuf", [128, TC], "float8_e4m3fn_x4"),
+    "xs": ("sbuf", [128, TC], "uint8"),
+    "ys": ("sbuf", [128, N * O * TC], "float32"),
+    "ps": ("psum", [128, 8 * 512], "float32"),
+}
+SEMAPHORES = ["ldc", "ld0", "ld1", "ldx", "lst", "sx", "sent", "st"]
+for _s in range(N):
+    SCRATCH["of%d" % _s] = ("sbuf", [128, C, 2 * NT, 16], "uint16")
+    for _c in range(C):
+        SCRATCH["a%d%d" % (_s, _c)] = ("sbuf", [128, NT * UC], "bfloat16")
+        SCRATCH["w%d%d" % (_s, _c)] = ("sbuf", [128, NT * UC], "bfloat16")
+        SCRATCH["q%d%d" % (_s, _c)] = ("sbuf", [128, UC], "float8_e4m3fn_x4")
+        SCRATCH["s%d%d" % (_s, _c)] = ("sbuf", [128, UC], "uint8")
+        SEMAPHORES += ["v%d%d" % (_s, _c), "q%d%d" % (_s, _c), "r%d%d" % (_s, _c), "l%d%d" % (_s, _c)]
+        SEMAPHORES += ["m%d%d0" % (_s, _c), "m%d%d1" % (_s, _c), "e%d%d" % (_s, _c)]
+        SEMAPHORES += ["a%d%d%d" % (_s, _c, _t) for _t in range(NT)]
+
+
+def relation(topo, a, b):
+    ca, cb = topo.chip(a), topo.chip(b)
+    return "mate" if topo.mates(ca, cb) else "plane" if topo.same_plane(ca, cb) else "diag"
+
+
+def helpers(topo, core, far):
+    own = [c for c in topo.cores_of(core) if c != core]
+    return sorted(own, key=lambda c: (topo.die(c) != topo.die(core), not topo.may_write(c, far)))
+
+
+def rank_program(g, core, T, topo):
+    S = T.sem
+    me = T.rank_of(core)
+    owner = me
+    if me is None:
+        for r in range(N):
+            if core in topo.cores_of(T.cores[r]):
+                owner = r
+        if owner is None:
+            return
+    rel = {r: relation(topo, T.cores[owner], T.cores[r]) for r in range(N) if r != owner}
+    by = {rel[r]: r for r in rel}
+    hs = helpers(topo, T.cores[owner], T.cores[by["mate"]])
+    near = topo.engines(T.cores[owner], hs[0])
+    if CFG["half"]:
+        near = [e for e in near if e not in topo.engines(T.cores[owner], T.cores[by["mate"]])]
+
+    def send(src, cores, sem):
+        es = near if cores[0] in hs else topo.engines(core, cores[0])
+        ids = [DstId(rid=topo.addr(c)[0], pnc=topo.addr(c)[1]) for c in cores]
+        g.remote_dma_fused([RemoteDMATransfer(dst_ids=ids, dma_engine_mask=sum(1 << e for e in es), remote_sem=sem, srcs=[src],
+                                              dsts=[src] * len(ids))], local_sem=S.sent)
+        return len(es)
+
+    def jobs():
+        out = [("l%d%d" % (owner, c), [T["of%d" % owner][:, c, :, :]], h, rs) for c in CFG["lists"] for h, rs in CFG["lists"][c]]
+        for c in range(C):
+            for h, rs in CFG["codes"].get(c, []):
+                out.append(("r%d%d" % (owner, c), [T["q%d%d" % (owner, c)][:, :].bitcast(dt.uint8), T["s%d%d" % (owner, c)][:, :]], h, rs))
+        return out
+
+    if me is None:
+        ns = 0
+        for w, c in CFG["so"]:
+            for sem, srcs, h, rs in jobs():
+                if sem == "%s%d%d" % (w, owner, c) and h is not None and hs[h] == core:
+                    g.wait_ge(S[sem], len(srcs) * len(near))
+                    for s in srcs:
+                        ns += send(s, [T.cores[by[k]] for k in rs], S[sem])
+        if ns:
+            g.wait_ge(S.sent, ns)
+        return
+    v, a, te, sy = g.vector, g.scalar, g.tensor, g.sync
+    sent_by = {k: [c for c in CFG["codes"] if any(k in rs for _, rs in CFG["codes"][c])] for k in by}
+    made = [(me, 0), (me, 1)]
+    got = []
+    for k in ("diag", "plane", "mate"):
+        made += [(by[k], c) for c in range(C) if c not in sent_by[k]]
+    for c in range(C):
+        got += [(by[k], c) for k in ("mate", "plane", "diag") if c in sent_by[k]]
+
+    sy.dma_start(T.cwb[:], T.cw[:, :]).then_inc(S.ldc, 16)
+    sy.dma_start(T.bk0[:, :], T.book[:, 0:NT * K]).then_inc(S.ld0, 16)
+    sy.dma_start(T.bk1[:, :], T.book[:, NT * K:2 * NT * K]).then_inc(S.ld1, 16)
+    sy.dma_start(T.xb[:, :], T.x[:, :]).then_inc(S.ldx, 16)
+
+    v.wait_ge(S.ldc, 16)
+    of = T["of%d" % me]
+    for m in range(2):
+        for t in range(NT):
+            v.tensor_scalar(of[:, :, m * NT + t, :], T.cwb[:, :, m, :], 4, t, AluOpType.mult, AluOpType.add).then_inc(S.lst, 1)
+    nlst = 2 * NT
+
+    nsent = 0
+    g.wait_ge(S.lst, nlst)
+    for w, c in CFG["so"]:
+        js = [j for j in jobs() if j[0] == "%s%d%d" % (w, me, c)]
+        if not js:
+            continue
+        if w == "r":
+            g.wait_ge(S["q%d%d" % (me, c)], 1)
+        for i in range(len(js[0][1])):
+            off = []
+            on = []
+            for sem, srcs, h, rs in js:
+                if h is None:
+                    off += [T.cores[by[k]] for k in rs]
+                else:
+                    on.append(hs[h])
+            sem, src = js[0][0], js[0][1][i]
+            for ds in (on, off):
+                if ds:
+                    nsent += send(src, ds, S[sem])
+    g.wait_ge(S.sent, nsent)
+
+    slots = [(4 * (k + 1) + CFG["lag"], 0, k, u) for k, u in enumerate(made)]
+    slots += [(CFG["gotpos"].get(i, 999), 1, i, u) for i, u in enumerate(got)]
+    slots.sort()
+    order = [u for _, _, _, u in slots]
+    col = lambda u: (u[0] * O + 2 * u[1]) * TC
+
+    def evac(k, h, e):
+        u = order[k]
+        src = T.ps[:, (2 * k + h) % 8 * 512:(2 * k + h) % 8 * 512 + TC]
+        dst = T.ys[:, col(u) + h * TC:col(u) + (h + 1) * TC]
+        sem = S["m%d%d%d" % (u + (h,))]
+        if CFG["evS"][2 * k + h] != e:
+            return
+        if e:
+            a.wait_ge(sem, 1)
+            a.activation(dst, src, ActivationFunctionType.Copy).then_inc(S["e%d%d" % u], 1)
+        else:
+            v.wait_ge(sem, 1)
+            v.tensor_copy(dst, src).then_inc(S["e%d%d" % u], 1)
+
+    dn = [0, 0]
+
+    def evacs(slot, e):
+        while dn[e] < len(order) and slots[dn[e]][0] <= slot:
+            evac(dn[e], 0, e)
+            evac(dn[e], 1, e)
+            dn[e] += 1
+
+    a.wait_ge(S.lst, nlst)
+    a.wait_ge(S.ld0, 16)
+    v.wait_ge(S.lst, nlst)
+    v.wait_ge(S.ld1, 16)
+    for k, u in enumerate(made):
+        s, c = u
+        of = T["of%d" % s]
+        ne = len(topo.engines(T.cores[s], core)) if s != me else 0
+        if s != me:
+            a.wait_ge(S["l%d%d" % u], ne)
+            v.wait_ge(S["l%d%d" % u], ne)
+        A, W = T["a%d%d" % u], T["w%d%d" % u]
+        for t in range(NT):
+            a.activation(A[:, t * UC:(t + 1) * UC], T.bk0[:, :].indirect(of[:, c, t, :]), ActivationFunctionType.Copy).then_inc(S["a%d%d%d" % (s, c, t)], 1)
+            evacs(4 * k + t - CFG["sl"], 1)
+        for t in range(NT):
+            v.wait_ge(S["a%d%d%d" % (s, c, t)], 1)
+            v.tensor_tensor(W[:, t:NT * UC:NT], T.bk1[:, :].indirect(of[:, c, NT + t, :]), A[:, t * UC:(t + 1) * UC], AluOpType.add).then_inc(S["v%d%d" % u], 1)
+            evacs(4 * k + t, 0)
+        v.wait_ge(S["v%d%d" % u], NT)
+        v.quantize_mx(T["q%d%d" % u][:, :], T["s%d%d" % u][:, :], W[:, :]).then_inc(S["q%d%d" % u], 1)
+        if k == 0:
+            v.wait_ge(S.ldx, 16)
+            v.quantize_mx(T.xq[:, :], T.xs[:, :], T.xb[:, :]).then_inc(S.sx, 1)
+    evacs(9999, 1)
+    evacs(9999, 0)
+
+    te.wait_ge(S.sx, 1)
+    for k, u in enumerate(order):
+        if u in made:
+            te.wait_ge(S["q%d%d" % u], 1)
+        else:
+            te.wait_ge(S["r%d%d" % u], 2 * len(topo.engines(T.cores[u[0]], core)))
+        if k >= 4:
+            te.wait_ge(S["e%d%d" % order[k - 4]], 2)
+        for h in range(2):
+            b = (2 * k + h) % 8 * 512
+            te.matmul_mx(T.ps[:, b:b + TC], T["q%d%d" % u][:, h * CW:(h + 1) * CW], T["s%d%d" % u][:, h * CW:(h + 1) * CW],
+                         T.xq[:, :], T.xs[:, :], True, True).then_inc(S["m%d%d%d" % (u + (h,))], 1)
+    for k, u in enumerate(order):
+        sy.wait_ge(S["e%d%d" % u], 2)
+        sy.dma_start(T.y[:, col(u):col(u) + 2 * TC], T.ys[:, col(u):col(u) + 2 * TC]).then_inc(S.st, 16)
+    sy.wait_ge(S.st, 16 * len(order))

@@ -6,15 +6,14 @@ CW = 128
 C = 2
 UC = 2 * CW
 NT = 4
-CFG = {
-    "codes": {0: [(None, ("mate", "plane"))], 1: [(None, ("mate",))]},
-    "lists": {0: [(None, ("diag",))], 1: [(None, ("plane", "diag"))]},
-    "gotpos": {0: 14, 1: 15, 2: 20},
-    "lag": 1, "sl": 2,
-    "evS": (1, 0, 1, 1, 1, 0, 1, 1, 1, 0, 1, 1, 1, 0, 0, 1),
-    "so": [("l", 0), ("l", 1), ("r", 0), ("r", 1)],
-    "half": 0,
-}
+
+PARTS = [("own", 0, 0, 1, 1), ("own", 0, 1, 1, 1), ("own", 1, 0, 2, 2), ("diag", 0, 0, 2, 2), ("diag", 1, 0, 2, 2)]
+ORDER = [("own", 0), ("own", 1), ("mate", 0), ("diag", 0), ("plane", 0), ("mate", 1), ("diag", 1), ("plane", 1)]
+SCALAR = [(0, 0), (0, 1), (0, 2), (0, 3), (1, 0), (1, 1), (1, 2), (1, 3), (2, 0), (2, 1), 0, 1, (3, 0), (3, 1), (4, 0), 2, 3, (4, 1),
+          4, 5, 6, 8, 9, 10, 13, 15]
+VECTOR = [(0, 0), (0, 1), (0, 2), (0, 3), (0, "q"), (1, 0), (1, 1), (1, 2), (1, 3), (1, "q"), "x",
+          (2, 0), (2, 1), "l", (2, 2), (2, 3), (2, "q"), (3, 0), (3, 1), (3, 2), (3, 3), (3, "q"),
+          (4, 0), (4, 1), (4, 2), 7, (4, 3), (4, "q"), 11, 12, 14]
 
 SCRATCH = {
     "cwb": ("sbuf", [128, O, 2, 8], "int32"),
@@ -26,17 +25,22 @@ SCRATCH = {
     "ys": ("sbuf", [128, N * O * TC], "float32"),
     "ps": ("psum", [128, 8 * 512], "float32"),
 }
-SEMAPHORES = ["ldc", "ld0", "ld1", "ldx", "lst", "sx", "sent", "st"]
+SEMAPHORES = ["ldc", "ld0", "ld1", "ldx", "lsti", "lstd", "sx", "sent", "st", "ha", "hb", "hc"]
+SEMAPHORES += ["lsta%d" % _t for _t in range(NT)]
 for _s in range(N):
-    SCRATCH["of%d" % _s] = ("sbuf", [128, C, 2 * NT, 16], "uint16")
+    SCRATCH["li%d" % _s] = ("sbuf", [128, C, 2, 16], "uint16")
+    SCRATCH["of%d" % _s] = ("sbuf", [128, C, 4, 32], "uint16")
+    SEMAPHORES += ["l%d" % _s]
     for _c in range(C):
         SCRATCH["a%d%d" % (_s, _c)] = ("sbuf", [128, NT * UC], "bfloat16")
         SCRATCH["w%d%d" % (_s, _c)] = ("sbuf", [128, NT * UC], "bfloat16")
         SCRATCH["q%d%d" % (_s, _c)] = ("sbuf", [128, UC], "float8_e4m3fn_x4")
         SCRATCH["s%d%d" % (_s, _c)] = ("sbuf", [128, UC], "uint8")
-        SEMAPHORES += ["v%d%d" % (_s, _c), "q%d%d" % (_s, _c), "r%d%d" % (_s, _c), "l%d%d" % (_s, _c)]
-        SEMAPHORES += ["m%d%d0" % (_s, _c), "m%d%d1" % (_s, _c), "e%d%d" % (_s, _c)]
-        SEMAPHORES += ["a%d%d%d" % (_s, _c, _t) for _t in range(NT)]
+        SEMAPHORES += ["r%d%d" % (_s, _c)]
+for _p in range(len(PARTS)):
+    SEMAPHORES += ["pa%d%d" % (_p, _t) for _t in range(NT)] + ["pv%d" % _p, "pq%d" % _p]
+for _k in range(N * O):
+    SEMAPHORES += ["m%d" % _k, "e%d" % _k]
 
 
 def relation(topo, a, b):
@@ -44,9 +48,8 @@ def relation(topo, a, b):
     return "mate" if topo.mates(ca, cb) else "plane" if topo.same_plane(ca, cb) else "diag"
 
 
-def helpers(topo, core, far):
-    own = [c for c in topo.cores_of(core) if c != core]
-    return sorted(own, key=lambda c: (topo.die(c) != topo.die(core), not topo.may_write(c, far)))
+def helper(topo, core, far):
+    return [c for c in topo.cores_of(core) if topo.die(c) != topo.die(core) and topo.may_write(c, far)][0]
 
 
 def rank_program(g, core, T, topo):
@@ -59,149 +62,152 @@ def rank_program(g, core, T, topo):
                 owner = r
         if owner is None:
             return
-    rel = {r: relation(topo, T.cores[owner], T.cores[r]) for r in range(N) if r != owner}
-    by = {rel[r]: r for r in rel}
-    hs = helpers(topo, T.cores[owner], T.cores[by["mate"]])
-    near = topo.engines(T.cores[owner], hs[0])
-    if CFG["half"]:
-        near = [e for e in near if e not in topo.engines(T.cores[owner], T.cores[by["mate"]])]
+    home = T.cores[owner]
+    by = {relation(topo, home, T.cores[r]): r for r in range(N) if r != owner}
+    at = {k: T.cores[by[k]] for k in by}
+    hlp = helper(topo, home, at["plane"])
 
-    def send(src, cores, sem):
-        es = near if cores[0] in hs else topo.engines(core, cores[0])
+    def transfer(src, cores, sem, es):
         ids = [DstId(rid=topo.addr(c)[0], pnc=topo.addr(c)[1]) for c in cores]
-        g.remote_dma_fused([RemoteDMATransfer(dst_ids=ids, dma_engine_mask=sum(1 << e for e in es), remote_sem=sem, srcs=[src],
-                                              dsts=[src] * len(ids))], local_sem=S.sent)
-        return len(es)
+        return RemoteDMATransfer(dst_ids=ids, dma_engine_mask=sum(1 << e for e in es), remote_sem=S[sem], srcs=[src],
+                                 dsts=[src] * len(ids))
 
-    def jobs():
-        out = [("l%d%d" % (owner, c), [T["of%d" % owner][:, c, :, :]], h, rs) for c in CFG["lists"] for h, rs in CFG["lists"][c]]
-        for c in range(C):
-            for h, rs in CFG["codes"].get(c, []):
-                out.append(("r%d%d" % (owner, c), [T["q%d%d" % (owner, c)][:, :].bitcast(dt.uint8), T["s%d%d" % (owner, c)][:, :]], h, rs))
-        return out
+    Q0, S0 = T["q%d0" % owner], T["s%d0" % owner]
+    early = [("ha", Q0[:, 0:CW].bitcast(dt.uint8)), ("hb", Q0[:, CW:UC].bitcast(dt.uint8)), ("hc", S0[:, :])]
+    far = topo.engines(home, at["mate"])
+    near = [e for e in topo.engines(home, hlp) if e not in far]
 
     if me is None:
-        ns = 0
-        for w, c in CFG["so"]:
-            for sem, srcs, h, rs in jobs():
-                if sem == "%s%d%d" % (w, owner, c) and h is not None and hs[h] == core:
-                    g.wait_ge(S[sem], len(srcs) * len(near))
-                    for s in srcs:
-                        ns += send(s, [T.cores[by[k]] for k in rs], S[sem])
-        if ns:
-            g.wait_ge(S.sent, ns)
+        if core == hlp:
+            es = topo.engines(core, at["plane"])
+            for sem, src in early:
+                g.wait_ge(S[sem], len(near))
+                g.remote_dma_fused([transfer(src, [at["plane"]], "r%d0" % owner, es)], local_sem=S.sent)
+            g.wait_ge(S.sent, len(early) * len(es))
         return
     v, a, te, sy = g.vector, g.scalar, g.tensor, g.sync
-    sent_by = {k: [c for c in CFG["codes"] if any(k in rs for _, rs in CFG["codes"][c])] for k in by}
-    made = [(me, 0), (me, 1)]
-    got = []
-    for k in ("diag", "plane", "mate"):
-        made += [(by[k], c) for c in range(C) if c not in sent_by[k]]
-    for c in range(C):
-        got += [(by[k], c) for k in ("mate", "plane", "diag") if c in sent_by[k]]
+    who = dict(by)
+    who["own"] = me
+    nfar = {w: len(topo.engines(T.cores[by[w]], core)) for w in by}
 
     sy.dma_start(T.cwb[:], T.cw[:, :]).then_inc(S.ldc, 16)
     sy.dma_start(T.bk0[:, :], T.book[:, 0:NT * K]).then_inc(S.ld0, 16)
     sy.dma_start(T.bk1[:, :], T.book[:, NT * K:2 * NT * K]).then_inc(S.ld1, 16)
     sy.dma_start(T.xb[:, :], T.x[:, :]).then_inc(S.ldx, 16)
 
-    v.wait_ge(S.ldc, 16)
-    of = T["of%d" % me]
-    for m in range(2):
+    def tables(s, sems):
         for t in range(NT):
-            v.tensor_scalar(of[:, :, m * NT + t, :], T.cwb[:, :, m, :], 4, t, AluOpType.mult, AluOpType.add).then_inc(S.lst, 1)
-    nlst = 2 * NT
+            v.tensor_scalar(T["of%d" % s][:, :, t // 2:4:2, 16 * (t % 2):16 * (t % 2) + 16], T["li%d" % s][:, :, :, :], t, None,
+                            AluOpType.add).then_inc(S[sems[t]], 1)
+
+    v.wait_ge(S.ldc, 16)
+    li = T["li%d" % me]
+    for m in range(2):
+        v.tensor_scalar(li[:, :, m, :], T.cwb[:, :, m, :], NT, None, AluOpType.mult).then_inc(S.lsti, 1)
+    v.wait_ge(S.lsti, 2)
+    tables(me, ["lsta%d" % t for t in range(NT)])
 
     nsent = 0
-    g.wait_ge(S.lst, nlst)
-    for w, c in CFG["so"]:
-        js = [j for j in jobs() if j[0] == "%s%d%d" % (w, me, c)]
-        if not js:
-            continue
-        if w == "r":
-            g.wait_ge(S["q%d%d" % (me, c)], 1)
-        for i in range(len(js[0][1])):
-            off = []
-            on = []
-            for sem, srcs, h, rs in js:
-                if h is None:
-                    off += [T.cores[by[k]] for k in rs]
-                else:
-                    on.append(hs[h])
-            sem, src = js[0][0], js[0][1][i]
-            for ds in (on, off):
-                if ds:
-                    nsent += send(src, ds, S[sem])
+    g.wait_ge(S.lsti, 2)
+    es = topo.engines(core, at["diag"])
+    g.remote_dma_fused([transfer(li[:, :, :, :], [at["diag"]], "l%d" % me, es)], local_sem=S.sent)
+    nsent += len(es)
+    for i, (sem, src) in enumerate(early):
+        if i < 2:
+            g.wait_ge(S["pq%d" % i], 1)
+        g.remote_dma_fused([transfer(src, [at["mate"]], "r%d0" % me, far), transfer(src, [hlp], sem, near)], local_sem=S.sent)
+        nsent += len(far) + len(near)
+    g.wait_ge(S.pq2, 1)
+    for src in (T["q%d1" % me][:, :].bitcast(dt.uint8), T["s%d1" % me][:, :]):
+        g.remote_dma_fused([transfer(src, [at["plane"], at["mate"]], "r%d1" % me, far)], local_sem=S.sent)
+        nsent += len(far)
     g.wait_ge(S.sent, nsent)
 
-    slots = [(4 * (k + 1) + CFG["lag"], 0, k, u) for k, u in enumerate(made)]
-    slots += [(CFG["gotpos"].get(i, 999), 1, i, u) for i, u in enumerate(got)]
-    slots.sort()
-    order = [u for _, _, _, u in slots]
-    col = lambda u: (u[0] * O + 2 * u[1]) * TC
+    def col(k):
+        w, c = ORDER[k // 2]
+        return (who[w] * O + 2 * c + k % 2) * TC
 
-    def evac(k, h, e):
-        u = order[k]
-        src = T.ps[:, (2 * k + h) % 8 * 512:(2 * k + h) % 8 * 512 + TC]
-        dst = T.ys[:, col(u) + h * TC:col(u) + (h + 1) * TC]
-        sem = S["m%d%d%d" % (u + (h,))]
-        if CFG["evS"][2 * k + h] != e:
-            return
-        if e:
-            a.wait_ge(sem, 1)
-            a.activation(dst, src, ActivationFunctionType.Copy).then_inc(S["e%d%d" % u], 1)
-        else:
-            v.wait_ge(sem, 1)
-            v.tensor_copy(dst, src).then_inc(S["e%d%d" % u], 1)
+    def take(k):
+        return T.ys[:, col(k):col(k) + TC], T.ps[:, k % 8 * 512:k % 8 * 512 + TC]
 
-    dn = [0, 0]
+    seen = {}
 
-    def evacs(slot, e):
-        while dn[e] < len(order) and slots[dn[e]][0] <= slot:
-            evac(dn[e], 0, e)
-            evac(dn[e], 1, e)
-            dn[e] += 1
+    def once(q, key, sem, n):
+        if (key, sem) not in seen:
+            seen[(key, sem)] = 1
+            q.wait_ge(S[sem], n)
 
-    a.wait_ge(S.lst, nlst)
     a.wait_ge(S.ld0, 16)
-    v.wait_ge(S.lst, nlst)
+    for it in SCALAR:
+        if isinstance(it, int):
+            a.wait_ge(S["m%d" % it], 1)
+            dst, src = take(it)
+            a.activation(dst, src, ActivationFunctionType.Copy).then_inc(S["e%d" % it], 1)
+            continue
+        p, i = it
+        w, c, h, nh, nt = PARTS[p]
+        s = who[w]
+        for t in range(i * nt, (i + 1) * nt):
+            if w == "own":
+                once(a, "a", "lsta%d" % t, 1)
+            else:
+                once(a, "a", "lstd", NT)
+        A, of = T["a%d%d" % (s, c)], T["of%d" % s]
+        t = i * nt
+        off = of[:, c, t // 2, :] if nt == 2 else of[:, c, t // 2, 16 * (t % 2) + 8 * h:16 * (t % 2) + 8 * (h + nh)]
+        a.activation(A[:, t * UC + h * CW:(t + nt - 1) * UC + (h + nh) * CW], T.bk0[:, :].indirect(off),
+                     ActivationFunctionType.Copy).then_inc(S["pa%d%d" % (p, i)], 1)
+
+    for t in range(NT):
+        v.wait_ge(S["lsta%d" % t], 1)
     v.wait_ge(S.ld1, 16)
-    for k, u in enumerate(made):
-        s, c = u
-        of = T["of%d" % s]
-        ne = len(topo.engines(T.cores[s], core)) if s != me else 0
-        if s != me:
-            a.wait_ge(S["l%d%d" % u], ne)
-            v.wait_ge(S["l%d%d" % u], ne)
-        A, W = T["a%d%d" % u], T["w%d%d" % u]
-        for t in range(NT):
-            a.activation(A[:, t * UC:(t + 1) * UC], T.bk0[:, :].indirect(of[:, c, t, :]), ActivationFunctionType.Copy).then_inc(S["a%d%d%d" % (s, c, t)], 1)
-            evacs(4 * k + t - CFG["sl"], 1)
-        for t in range(NT):
-            v.wait_ge(S["a%d%d%d" % (s, c, t)], 1)
-            v.tensor_tensor(W[:, t:NT * UC:NT], T.bk1[:, :].indirect(of[:, c, NT + t, :]), A[:, t * UC:(t + 1) * UC], AluOpType.add).then_inc(S["v%d%d" % u], 1)
-            evacs(4 * k + t, 0)
-        v.wait_ge(S["v%d%d" % u], NT)
-        v.quantize_mx(T["q%d%d" % u][:, :], T["s%d%d" % u][:, :], W[:, :]).then_inc(S["q%d%d" % u], 1)
-        if k == 0:
+    for it in VECTOR:
+        if it == "x":
             v.wait_ge(S.ldx, 16)
             v.quantize_mx(T.xq[:, :], T.xs[:, :], T.xb[:, :]).then_inc(S.sx, 1)
-    evacs(9999, 1)
-    evacs(9999, 0)
+            continue
+        if it == "l":
+            v.wait_ge(S["l%d" % by["diag"]], nfar["diag"])
+            tables(by["diag"], ["lstd"] * NT)
+            continue
+        if isinstance(it, int):
+            v.wait_ge(S["m%d" % it], 1)
+            dst, src = take(it)
+            v.tensor_copy(dst, src).then_inc(S["e%d" % it], 1)
+            continue
+        p, t = it
+        w, c, h, nh, nt = PARTS[p]
+        s = who[w]
+        A, W, of = T["a%d%d" % (s, c)], T["w%d%d" % (s, c)], T["of%d" % s]
+        lo, hi = h * CW, (h + nh) * CW
+        if t == "q":
+            v.wait_ge(S["pv%d" % p], NT)
+            v.quantize_mx(T["q%d%d" % (s, c)][:, lo:hi], T["s%d%d" % (s, c)][:, lo:hi], W[:, NT * lo:NT * hi]).then_inc(S["pq%d" % p], 1)
+            continue
+        if w != "own":
+            once(v, "v", "lstd", NT)
+        once(v, "v", "pa%d%d" % (p, t // nt), 1)
+        off = of[:, c, 2 + t // 2, 16 * (t % 2) + 8 * h:16 * (t % 2) + 8 * (h + nh)]
+        v.tensor_tensor(W[:, NT * lo + t:NT * hi:NT], T.bk1[:, :].indirect(off), A[:, t * UC + lo:t * UC + hi],
+                        AluOpType.add).then_inc(S["pv%d" % p], 1)
 
     te.wait_ge(S.sx, 1)
-    for k, u in enumerate(order):
-        if u in made:
-            te.wait_ge(S["q%d%d" % u], 1)
+    for k in range(N * O):
+        w, c = ORDER[k // 2]
+        h = k % 2
+        s = who[w]
+        if w in ("own", "diag"):
+            for p, (w2, c2, h2, nh, nt) in enumerate(PARTS):
+                if (w2, c2) == (w, c) and h2 <= h < h2 + nh:
+                    once(te, "t", "pq%d" % p, 1)
         else:
-            te.wait_ge(S["r%d%d" % u], 2 * len(topo.engines(T.cores[u[0]], core)))
-        if k >= 4:
-            te.wait_ge(S["e%d%d" % order[k - 4]], 2)
-        for h in range(2):
-            b = (2 * k + h) % 8 * 512
-            te.matmul_mx(T.ps[:, b:b + TC], T["q%d%d" % u][:, h * CW:(h + 1) * CW], T["s%d%d" % u][:, h * CW:(h + 1) * CW],
-                         T.xq[:, :], T.xs[:, :], True, True).then_inc(S["m%d%d%d" % (u + (h,))], 1)
-    for k, u in enumerate(order):
-        sy.wait_ge(S["e%d%d" % u], 2)
-        sy.dma_start(T.y[:, col(u):col(u) + 2 * TC], T.ys[:, col(u):col(u) + 2 * TC]).then_inc(S.st, 16)
-    sy.wait_ge(S.st, 16 * len(order))
+            once(te, "t", "r%d%d" % (s, c), (len(early) if c == 0 else 2) * nfar[w])
+        if k >= 8:
+            te.wait_ge(S["e%d" % (k - 8)], 1)
+        te.matmul_mx(T.ps[:, k % 8 * 512:k % 8 * 512 + TC], T["q%d%d" % (s, c)][:, h * CW:(h + 1) * CW],
+                     T["s%d%d" % (s, c)][:, h * CW:(h + 1) * CW], T.xq[:, :], T.xs[:, :], True, True).then_inc(S["m%d" % k], 1)
+    for k in range(0, N * O, 2):
+        sy.wait_ge(S["e%d" % k], 1)
+        sy.wait_ge(S["e%d" % (k + 1)], 1)
+        sy.dma_start(T.y[:, col(k):col(k) + 2 * TC], T.ys[:, col(k):col(k) + 2 * TC]).then_inc(S.st, 16)
+    sy.wait_ge(S.st, 16 * (N * O // 2))

from concourse.bass import DstId, RemoteDMATransfer
from concourse.mybir import dt, AluOpType, ActivationFunctionType

N, TC, O, K = 4, 256, 4, 256
CW = 128
C = 2
UC = 2 * CW
NT = 4

PARTS = [("own", 0, 0, 1, 1), ("own", 0, 1, 1, 1), ("own", 1, 0, 2, 2), ("diag", 0, 0, 2, 2), ("diag", 1, 0, 2, 2)]
ORDER = [("own", 0), ("own", 1), ("mate", 0), ("diag", 0), ("plane", 0), ("mate", 1), ("diag", 1), ("plane", 1)]
SCALAR = [(0, 0), (0, 1), (0, 2), (0, 3), (1, 0), (1, 1), (1, 2), (1, 3), (2, 0), (2, 1), 0, 1, (3, 0), (3, 1), (4, 0), 2, 3, (4, 1),
          4, 5, 6, 8, 9, 10, 13, 15]
VECTOR = [(0, 0), (0, 1), (0, 2), (0, 3), (0, "q"), (1, 0), (1, 1), (1, 2), (1, 3), (1, "q"), "x",
          (2, 0), (2, 1), "l", (2, 2), (2, 3), (2, "q"), (3, 0), (3, 1), (3, 2), (3, 3), (3, "q"),
          (4, 0), (4, 1), (4, 2), 7, (4, 3), (4, "q"), 11, 12, 14]

SCRATCH = {
    "cwb": ("sbuf", [128, O, 2, 8], "int32"),
    "bk0": ("sbuf", [128, NT * K], "bfloat16"),
    "bk1": ("sbuf", [128, NT * K], "bfloat16"),
    "xb": ("sbuf", [128, NT * TC], "bfloat16"),
    "xq": ("sbuf", [128, TC], "float8_e4m3fn_x4"),
    "xs": ("sbuf", [128, TC], "uint8"),
    "ys": ("sbuf", [128, N * O * TC], "float32"),
    "ps": ("psum", [128, 8 * 512], "float32"),
}
SEMAPHORES = ["ldc", "ld0", "ld1", "ldx", "lsti", "lstd", "sx", "sent", "st", "ha", "hb", "hc"]
SEMAPHORES += ["lsta%d" % _t for _t in range(NT)]
for _s in range(N):
    SCRATCH["li%d" % _s] = ("sbuf", [128, C, 2, 16], "uint16")
    SCRATCH["of%d" % _s] = ("sbuf", [128, C, 4, 32], "uint16")
    SEMAPHORES += ["l%d" % _s]
    for _c in range(C):
        SCRATCH["a%d%d" % (_s, _c)] = ("sbuf", [128, NT * UC], "bfloat16")
        SCRATCH["w%d%d" % (_s, _c)] = ("sbuf", [128, NT * UC], "bfloat16")
        SCRATCH["q%d%d" % (_s, _c)] = ("sbuf", [128, UC], "float8_e4m3fn_x4")
        SCRATCH["s%d%d" % (_s, _c)] = ("sbuf", [128, UC], "uint8")
        SEMAPHORES += ["r%d%d" % (_s, _c)]
for _p in range(len(PARTS)):
    SEMAPHORES += ["pa%d%d" % (_p, _t) for _t in range(NT)] + ["pv%d" % _p, "pq%d" % _p]
for _k in range(N * O):
    SEMAPHORES += ["m%d" % _k, "e%d" % _k]


def relation(topo, a, b):
    ca, cb = topo.chip(a), topo.chip(b)
    return "mate" if topo.mates(ca, cb) else "plane" if topo.same_plane(ca, cb) else "diag"


def helper(topo, core, far):
    return [c for c in topo.cores_of(core) if topo.die(c) != topo.die(core) and topo.may_write(c, far)][0]


def rank_program(g, core, T, topo):
    S = T.sem
    me = T.rank_of(core)
    owner = me
    if me is None:
        for r in range(N):
            if core in topo.cores_of(T.cores[r]):
                owner = r
        if owner is None:
            return
    home = T.cores[owner]
    by = {relation(topo, home, T.cores[r]): r for r in range(N) if r != owner}
    at = {k: T.cores[by[k]] for k in by}
    hlp = helper(topo, home, at["plane"])

    def transfer(src, cores, sem, es):
        ids = [DstId(rid=topo.addr(c)[0], pnc=topo.addr(c)[1]) for c in cores]
        return RemoteDMATransfer(dst_ids=ids, dma_engine_mask=sum(1 << e for e in es), remote_sem=S[sem], srcs=[src],
                                 dsts=[src] * len(ids))

    Q0, S0 = T["q%d0" % owner], T["s%d0" % owner]
    early = [("ha", Q0[:, 0:CW].bitcast(dt.uint8)), ("hb", Q0[:, CW:UC].bitcast(dt.uint8)), ("hc", S0[:, :])]
    far = topo.engines(home, at["mate"])
    near = [e for e in topo.engines(home, hlp) if e not in far]

    if me is None:
        if core == hlp:
            es = topo.engines(core, at["plane"])
            for sem, src in early:
                g.wait_ge(S[sem], len(near))
                g.remote_dma_fused([transfer(src, [at["plane"]], "r%d0" % owner, es)], local_sem=S.sent)
            g.wait_ge(S.sent, len(early) * len(es))
        return
    v, a, te, sy = g.vector, g.scalar, g.tensor, g.sync
    who = dict(by)
    who["own"] = me
    nfar = {w: len(topo.engines(T.cores[by[w]], core)) for w in by}

    sy.dma_start(T.cwb[:], T.cw[:, :]).then_inc(S.ldc, 16)
    sy.dma_start(T.bk0[:, :], T.book[:, 0:NT * K]).then_inc(S.ld0, 16)
    sy.dma_start(T.bk1[:, :], T.book[:, NT * K:2 * NT * K]).then_inc(S.ld1, 16)
    sy.dma_start(T.xb[:, :], T.x[:, :]).then_inc(S.ldx, 16)

    def tables(s, sems):
        for t in range(NT):
            v.tensor_scalar(T["of%d" % s][:, :, t // 2:4:2, 16 * (t % 2):16 * (t % 2) + 16], T["li%d" % s][:, :, :, :], t, None,
                            AluOpType.add).then_inc(S[sems[t]], 1)

    v.wait_ge(S.ldc, 16)
    li = T["li%d" % me]
    for m in range(2):
        v.tensor_scalar(li[:, :, m, :], T.cwb[:, :, m, :], NT, None, AluOpType.mult).then_inc(S.lsti, 1)
    v.wait_ge(S.lsti, 2)
    tables(me, ["lsta%d" % t for t in range(NT)])

    nsent = 0
    g.wait_ge(S.lsti, 2)
    es = topo.engines(core, at["diag"])
    g.remote_dma_fused([transfer(li[:, :, :, :], [at["diag"]], "l%d" % me, es)], local_sem=S.sent)
    nsent += len(es)
    for i, (sem, src) in enumerate(early):
        if i < 2:
            g.wait_ge(S["pq%d" % i], 1)
        g.remote_dma_fused([transfer(src, [at["mate"]], "r%d0" % me, far), transfer(src, [hlp], sem, near)], local_sem=S.sent)
        nsent += len(far) + len(near)
    g.wait_ge(S.pq2, 1)
    for src in (T["q%d1" % me][:, :].bitcast(dt.uint8), T["s%d1" % me][:, :]):
        g.remote_dma_fused([transfer(src, [at["plane"], at["mate"]], "r%d1" % me, far)], local_sem=S.sent)
        nsent += len(far)
    g.wait_ge(S.sent, nsent)

    def col(k):
        w, c = ORDER[k // 2]
        return (who[w] * O + 2 * c + k % 2) * TC

    def take(k):
        return T.ys[:, col(k):col(k) + TC], T.ps[:, k % 8 * 512:k % 8 * 512 + TC]

    seen = {}

    def once(q, key, sem, n):
        if (key, sem) not in seen:
            seen[(key, sem)] = 1
            q.wait_ge(S[sem], n)

    a.wait_ge(S.ld0, 16)
    for it in SCALAR:
        if isinstance(it, int):
            a.wait_ge(S["m%d" % it], 1)
            dst, src = take(it)
            a.activation(dst, src, ActivationFunctionType.Copy).then_inc(S["e%d" % it], 1)
            continue
        p, i = it
        w, c, h, nh, nt = PARTS[p]
        s = who[w]
        for t in range(i * nt, (i + 1) * nt):
            if w == "own":
                once(a, "a", "lsta%d" % t, 1)
            else:
                once(a, "a", "lstd", NT)
        A, of = T["a%d%d" % (s, c)], T["of%d" % s]
        t = i * nt
        off = of[:, c, t // 2, :] if nt == 2 else of[:, c, t // 2, 16 * (t % 2) + 8 * h:16 * (t % 2) + 8 * (h + nh)]
        a.activation(A[:, t * UC + h * CW:(t + nt - 1) * UC + (h + nh) * CW], T.bk0[:, :].indirect(off),
                     ActivationFunctionType.Copy).then_inc(S["pa%d%d" % (p, i)], 1)

    for t in range(NT):
        v.wait_ge(S["lsta%d" % t], 1)
    v.wait_ge(S.ld1, 16)
    for it in VECTOR:
        if it == "x":
            v.wait_ge(S.ldx, 16)
            v.quantize_mx(T.xq[:, :], T.xs[:, :], T.xb[:, :]).then_inc(S.sx, 1)
            continue
        if it == "l":
            v.wait_ge(S["l%d" % by["diag"]], nfar["diag"])
            tables(by["diag"], ["lstd"] * NT)
            continue
        if isinstance(it, int):
            v.wait_ge(S["m%d" % it], 1)
            dst, src = take(it)
            v.tensor_copy(dst, src).then_inc(S["e%d" % it], 1)
            continue
        p, t = it
        w, c, h, nh, nt = PARTS[p]
        s = who[w]
        A, W, of = T["a%d%d" % (s, c)], T["w%d%d" % (s, c)], T["of%d" % s]
        lo, hi = h * CW, (h + nh) * CW
        if t == "q":
            v.wait_ge(S["pv%d" % p], NT)
            v.quantize_mx(T["q%d%d" % (s, c)][:, lo:hi], T["s%d%d" % (s, c)][:, lo:hi], W[:, NT * lo:NT * hi]).then_inc(S["pq%d" % p], 1)
            continue
        if w != "own":
            once(v, "v", "lstd", NT)
        once(v, "v", "pa%d%d" % (p, t // nt), 1)
        off = of[:, c, 2 + t // 2, 16 * (t % 2) + 8 * h:16 * (t % 2) + 8 * (h + nh)]
        v.tensor_tensor(W[:, NT * lo + t:NT * hi:NT], T.bk1[:, :].indirect(off), A[:, t * UC + lo:t * UC + hi],
                        AluOpType.add).then_inc(S["pv%d" % p], 1)

    te.wait_ge(S.sx, 1)
    for k in range(N * O):
        w, c = ORDER[k // 2]
        h = k % 2
        s = who[w]
        if w in ("own", "diag"):
            for p, (w2, c2, h2, nh, nt) in enumerate(PARTS):
                if (w2, c2) == (w, c) and h2 <= h < h2 + nh:
                    once(te, "t", "pq%d" % p, 1)
        else:
            once(te, "t", "r%d%d" % (s, c), (len(early) if c == 0 else 2) * nfar[w])
        if k >= 8:
            te.wait_ge(S["e%d" % (k - 8)], 1)
        te.matmul_mx(T.ps[:, k % 8 * 512:k % 8 * 512 + TC], T["q%d%d" % (s, c)][:, h * CW:(h + 1) * CW],
                     T["s%d%d" % (s, c)][:, h * CW:(h + 1) * CW], T.xq[:, :], T.xs[:, :], True, True).then_inc(S["m%d" % k], 1)
    for k in range(0, N * O, 2):
        sy.wait_ge(S["e%d" % k], 1)
        sy.wait_ge(S["e%d" % (k + 1)], 1)
        sy.dma_start(T.y[:, col(k):col(k) + 2 * TC], T.ys[:, col(k):col(k) + 2 * TC]).then_inc(S.st, 16)
    sy.wait_ge(S.st, 16 * (N * O // 2))
